import numpy as np, ml_dtypes
CORES = [35,38,43,46]
N = 4
import mx_ref
NC, WT = 128, 2
BF = ml_dtypes.bfloat16
def pk(c, s, i=0):
    return (np.ascontiguousarray(c[:, 512 * i:512 * i + 512]), mx_ref.live(s[:, 128 * i:128 * i + 128]))
def inputs(rng, e, E):
    def f(*shape):
        v = (rng.standard_normal(shape, dtype=np.float32) * np.exp2(rng.integers(-2, 3, shape[:-1] + (1,)))).astype(BF)
        return mx_ref.spread((v.astype(np.float32) * np.exp2(rng.integers(-E, E + 1, shape[:-2] + (1, 1))).astype(np.float32)).astype(BF), rng, e)
    def packed(k):
        c = np.zeros((N, 128, k * 512), np.uint8); s = np.zeros((N, 128, k * 128), np.uint8)
        for r in range(N):
            for i in range(k):
                a, b = mx_ref.quantize(f(128, 512)); c[r][:, 512 * i:512 * i + 512] = a; s[r][:, 128 * i:128 * i + 128] = mx_ref.plane(b, rng)
        return c, s
    d = {}
    d["wc"], d["ws"] = packed(WT)
    d["x"] = f(N, 128, 4 * NC)
    return d
def setup_inputs(rng):
    return inputs(rng, 0, 0)
def setup_inputs_blocks(rng):
    return inputs(rng, 4, 0)
def setup_inputs_wide(rng):
    return inputs(rng, 0, 8)
def reference(wc, ws, x):
    y = np.zeros((N, 128, N * WT * NC), np.float32)
    for r in range(N):
        X = mx_ref.quantize(x[r])
        for b in range(N * WT):
            y[r][:, NC * b:NC * b + NC] = mx_ref.matmul(pk(wc[b // WT], ws[b // WT], b % WT), X)
    return {"y": y}

@@ -1,0 +1,156 @@
+from concourse.bass import DstId, RemoteDMATransfer
+from concourse.mybir import dt, ActivationFunctionType
+
+N, WT, NC = 4, 2, 128
+PW = WT * NC
+BANK = 512
+
+SCRATCH = {
+    "wq": ("sbuf", [128, N * PW], "float8_e4m3fn_x4"),
+    "wp": ("sbuf", [128, N * PW], "uint8"),
+    "xb": ("sbuf", [128, 4 * NC], "bfloat16"),
+    "xq": ("sbuf", [128, NC], "float8_e4m3fn_x4"),
+    "xp": ("sbuf", [128, NC], "uint8"),
+    "ps": ("psum", [128, BANK * N * WT], "float32"),
+    "yb": ("sbuf", [128, N * PW], "float32"),
+}
+SEMAPHORES = (["lwc", "lws", "lx", "q", "sent", "sts", "stc"]
+              + ["a%d" % j for j in range(N)]
+              + ["m%d" % b for b in range(N * WT)]
+              + ["cp%d" % j for j in range(N)])
+
+
+def _engines(mask):
+    return [e for e in range(mask.bit_length()) if (mask >> e) & 1]
+
+
+def _mask_of(engs):
+    n = 1
+    while 2 * n <= min(len(engs), 128):
+        n *= 2
+    m = 0
+    for e in engs[:n]:
+        m |= 1 << e
+    return m, n
+
+
+def _split(core, cores, topo):
+    others = [c for c in cores if c != core]
+    near = [c for c in others if topo.chip(c) == topo.chip(core)]
+    far = [c for c in others if topo.chip(c) != topo.chip(core)]
+    far.sort(key=lambda c: topo.die(c) != topo.die(core))
+    return near, far
+
+
+def _plan(src, cores, topo):
+    near, far = _split(src, cores, topo)
+    plan, taken = [], 0
+    if far:
+        allowed = topo.mask(src, far[0])
+        for c in far:
+            assert topo.may_write(src, c)
+            allowed &= topo.mask(src, c)
+        m, n = _mask_of(_engines(allowed))
+        plan.append((far, m, n))
+        taken = m
+    if near:
+        allowed = topo.mask(src, near[0])
+        for c in near:
+            allowed &= topo.mask(src, c)
+        m, n = _mask_of(_engines(allowed & ~taken))
+        plan.append((near, m, n))
+    return plan
+
+
+def rank_program(g, core, T, topo):
+    rank = T.rank_of(core)
+    if rank is None:
+        return
+    cores = list(T.cores)
+    sem = T.sem
+    near, far = _split(core, cores, topo)
+    lo, hi = PW * rank, PW * rank + PW
+
+    g.scalar.dma_start(T.wp[:, lo:hi], T.ws[:]).then_inc(sem.lws, 16)
+    g.sync.dma_start(T.wq[:, lo:hi].bitcast(dt.uint8), T.wc[:]).then_inc(sem.lwc, 16)
+    g.scalar.dma_start(T.xb[:], T.x[:]).then_inc(sem.lx, 16)
+
+    plan = _plan(core, cores, topo)
+
+    def send(view):
+        trs = []
+        for dests, m, _n in plan:
+            ids = []
+            for c in dests:
+                rid, pid, _se = topo.addr(c)
+                ids.append(DstId(rid=rid, pnc=pid))
+            trs.append(RemoteDMATransfer(dst_ids=ids, dma_engine_mask=m, remote_sem=sem["a%d" % rank],
+                                         srcs=[view], dsts=[view for _c in dests]))
+        g.remote_dma_fused(trs, local_sem=sem.sent)
+
+    g.wait_ge(sem.lws, 16)
+    send(T.wp[:, lo:hi])
+    g.wait_ge(sem.lwc, 16)
+    send(T.wq[:, lo:hi].bitcast(dt.uint8))
+
+    g.vector.wait_ge(sem.lx, 16)
+    g.vector.quantize_mx(T.xq[:], T.xp[:], T.xb[:]).then_inc(sem.q, 1)
+
+    order = [rank] + [T.rank_of(c) for c in near] + [T.rank_of(c) for c in far]
+
+    def landed(j):
+        for dests, _m, n in _plan(cores[j], cores, topo):
+            if core in dests:
+                return 2 * n
+        return 0
+
+    g.tensor.wait_ge(sem.lws, 16)
+    g.tensor.wait_ge(sem.lwc, 16)
+    g.tensor.wait_ge(sem.q, 1)
+    for j in order:
+        if j != rank:
+            g.tensor.wait_ge(sem["a%d" % j], landed(j))
+        for i in range(WT):
+            b = WT * j + i
+            g.tensor.matmul_mx(T.ps[:, BANK * b:BANK * b + NC], T.wq[:, NC * b:NC * b + NC], T.wp[:, NC * b:NC * b + NC],
+                               T.xq[:], T.xp[:], True, True).then_inc(sem["m%d" % b], 1)
+
+    groups = [[rank]]
+    for c in near:
+        j = T.rank_of(c)
+        if j == min(groups[0]) - 1 or j == max(groups[0]) + 1:
+            groups[0].append(j)
+        else:
+            groups.append([j])
+    for c in far:
+        groups.append([T.rank_of(c)])
+    last = groups[-1][-1]
+
+    for j in order:
+        for i in range(WT):
+            b = WT * j + i
+            src, dst = T.ps[:, BANK * b:BANK * b + NC], T.yb[:, NC * b:NC * b + NC]
+            if i % 2 == 0:
+                g.vector.wait_ge(sem["m%d" % b], 1)
+                g.vector.tensor_copy(dst, src).then_inc(sem["cp%d" % j], 1)
+            else:
+                g.scalar.wait_ge(sem["m%d" % b], 1)
+                g.scalar.activation(dst, src, ActivationFunctionType.Copy).then_inc(sem["cp%d" % j], 1)
+
+    n_sync = 0
+    for grp in groups:
+        a, z = PW * min(grp), PW * max(grp) + PW
+        if last in grp:
+            for j in grp:
+                g.scalar.wait_ge(sem["cp%d" % j], WT)
+            g.scalar.dma_start(T.y[:, a:z], T.yb[:, a:z]).then_inc(sem.stc, 16)
+        else:
+            for j in grp:
+                g.sync.wait_ge(sem["cp%d" % j], WT)
+            g.sync.dma_start(T.y[:, a:z], T.yb[:, a:z]).then_inc(sem.sts, 16)
+            n_sync += 1
+    if n_sync:
+        g.sync.wait_ge(sem.sts, 16 * n_sync)
+    g.scalar.wait_ge(sem.stc, 16)
+
+    g.wait_ge(sem.sent, 2 * sum(n for _d, _m, n in plan))

@@ -16,6 +16,7 @@ SCRATCH = {
 }
 SEMAPHORES = (["lwc", "lws", "lx", "q", "sent", "sts", "stc"]
               + ["a%d" % j for j in range(N)]
+              + ["p%d" % j for j in range(N)]
               + ["m%d" % b for b in range(N * WT)]
               + ["cp%d" % j for j in range(N)])
 
@@ -42,24 +43,21 @@ def _split(core, cores, topo):
     return near, far
 
 
-def _plan(src, cores, topo):
+def _masks(src, cores, topo):
     near, far = _split(src, cores, topo)
-    plan, taken = [], 0
+    fm, fn, nm, nn = 0, 0, 0, 0
     if far:
         allowed = topo.mask(src, far[0])
         for c in far:
             assert topo.may_write(src, c)
             allowed &= topo.mask(src, c)
-        m, n = _mask_of(_engines(allowed))
-        plan.append((far, m, n))
-        taken = m
+        fm, fn = _mask_of(_engines(allowed))
     if near:
         allowed = topo.mask(src, near[0])
         for c in near:
             allowed &= topo.mask(src, c)
-        m, n = _mask_of(_engines(allowed & ~taken))
-        plan.append((near, m, n))
-    return plan
+        nm, nn = _mask_of(_engines(allowed & ~fm))
+    return fm, fn, nm, nn
 
 
 def rank_program(g, core, T, topo):
@@ -69,29 +67,41 @@ def rank_program(g, core, T, topo):
     cores = list(T.cores)
     sem = T.sem
     near, far = _split(core, cores, topo)
+    fm, fn, nm, nn = _masks(core, cores, topo)
     lo, hi = PW * rank, PW * rank + PW
 
-    g.scalar.dma_start(T.wp[:, lo:hi], T.ws[:]).then_inc(sem.lws, 16)
+    g.sync.dma_start(T.wp[:, lo:hi], T.ws[:]).then_inc(sem.lws, 16)
     g.sync.dma_start(T.wq[:, lo:hi].bitcast(dt.uint8), T.wc[:]).then_inc(sem.lwc, 16)
-    g.scalar.dma_start(T.xb[:], T.x[:]).then_inc(sem.lx, 16)
+    g.sync.dma_start(T.xb[:], T.x[:]).then_inc(sem.lx, 16)
 
-    plan = _plan(core, cores, topo)
+    sent = [0]
 
-    def send(view):
+    def send(view, parts, rsem):
         trs = []
-        for dests, m, _n in plan:
+        for dests, m, n in parts:
             ids = []
             for c in dests:
                 rid, pid, _se = topo.addr(c)
                 ids.append(DstId(rid=rid, pnc=pid))
-            trs.append(RemoteDMATransfer(dst_ids=ids, dma_engine_mask=m, remote_sem=sem["a%d" % rank],
+            trs.append(RemoteDMATransfer(dst_ids=ids, dma_engine_mask=m, remote_sem=rsem,
                                          srcs=[view], dsts=[view for _c in dests]))
+            sent[0] += n
         g.remote_dma_fused(trs, local_sem=sem.sent)
 
     g.wait_ge(sem.lws, 16)
-    send(T.wp[:, lo:hi])
+    send(T.wp[:, lo:hi], [(far[:1], fm, fn), (near, nm, nn)], sem["p%d" % rank])
     g.wait_ge(sem.lwc, 16)
-    send(T.wq[:, lo:hi].bitcast(dt.uint8))
+    send(T.wq[:, lo:hi].bitcast(dt.uint8), [(far, fm, fn), (near, nm, nn)], sem["a%d" % rank])
+
+    for j, c in enumerate(cores):
+        if c == core:
+            continue
+        _nj, fj = _split(c, cores, topo)
+        if fj and fj[0] == core and fj[1:]:
+            for d in fj[1:]:
+                assert topo.chip(d) == topo.chip(core)
+            g.wait_ge(sem["p%d" % j], _masks(c, cores, topo)[1])
+            send(T.wp[:, PW * j:PW * j + PW], [(fj[1:], nm, nn)], sem["p%d" % j])
 
     g.vector.wait_ge(sem.lx, 16)
     g.vector.quantize_mx(T.xq[:], T.xp[:], T.xb[:]).then_inc(sem.q, 1)
@@ -99,31 +109,29 @@ def rank_program(g, core, T, topo):
     order = [rank] + [T.rank_of(c) for c in near] + [T.rank_of(c) for c in far]
 
     def landed(j):
-        for dests, _m, n in _plan(cores[j], cores, topo):
-            if core in dests:
-                return 2 * n
-        return 0
+        c = cores[j]
+        nj, fj = _split(c, cores, topo)
+        jfm, jfn, jnm, jnn = _masks(c, cores, topo)
+        if core in nj:
+            return jnn, jnn
+        if core == fj[0]:
+            return jfn, jfn
+        return jfn, _masks(fj[0], cores, topo)[3]
 
     g.tensor.wait_ge(sem.lws, 16)
     g.tensor.wait_ge(sem.lwc, 16)
     g.tensor.wait_ge(sem.q, 1)
     for j in order:
         if j != rank:
-            g.tensor.wait_ge(sem["a%d" % j], landed(j))
+            na, np_ = landed(j)
+            g.tensor.wait_ge(sem["p%d" % j], np_)
+            g.tensor.wait_ge(sem["a%d" % j], na)
         for i in range(WT):
             b = WT * j + i
             g.tensor.matmul_mx(T.ps[:, BANK * b:BANK * b + NC], T.wq[:, NC * b:NC * b + NC], T.wp[:, NC * b:NC * b + NC],
                                T.xq[:], T.xp[:], True, True).then_inc(sem["m%d" % b], 1)
 
-    groups = [[rank]]
-    for c in near:
-        j = T.rank_of(c)
-        if j == min(groups[0]) - 1 or j == max(groups[0]) + 1:
-            groups[0].append(j)
-        else:
-            groups.append([j])
-    for c in far:
-        groups.append([T.rank_of(c)])
+    groups = [[rank]] + [[T.rank_of(c)] for c in near] + [[T.rank_of(c)] for c in far]
     last = groups[-1][-1]
 
     for j in order:
@@ -153,4 +161,4 @@ def rank_program(g, core, T, topo):
         g.sync.wait_ge(sem.sts, 16 * n_sync)
     g.scalar.wait_ge(sem.stc, 16)
 
-    g.wait_ge(sem.sent, 2 * sum(n for _d, _m, n in plan))
+    g.wait_ge(sem.sent, sent[0])

from concourse.bass import DstId, RemoteDMATransfer
from concourse.mybir import dt, ActivationFunctionType

N, WT, NC = 4, 2, 128
PW = WT * NC
BANK = 512

SCRATCH = {
    "wq": ("sbuf", [128, N * PW], "float8_e4m3fn_x4"),
    "wp": ("sbuf", [128, N * PW], "uint8"),
    "xb": ("sbuf", [128, 4 * NC], "bfloat16"),
    "xq": ("sbuf", [128, NC], "float8_e4m3fn_x4"),
    "xp": ("sbuf", [128, NC], "uint8"),
    "ps": ("psum", [128, BANK * N * WT], "float32"),
    "yb": ("sbuf", [128, N * PW], "float32"),
}
SEMAPHORES = (["lwc", "lws", "lx", "q", "sent", "sts", "stc"]
              + ["a%d" % j for j in range(N)]
              + ["p%d" % j for j in range(N)]
              + ["m%d" % b for b in range(N * WT)]
              + ["cp%d" % j for j in range(N)])


def _engines(mask):
    return [e for e in range(mask.bit_length()) if (mask >> e) & 1]


def _mask_of(engs):
    n = 1
    while 2 * n <= min(len(engs), 128):
        n *= 2
    m = 0
    for e in engs[:n]:
        m |= 1 << e
    return m, n


def _split(core, cores, topo):
    others = [c for c in cores if c != core]
    near = [c for c in others if topo.chip(c) == topo.chip(core)]
    far = [c for c in others if topo.chip(c) != topo.chip(core)]
    far.sort(key=lambda c: topo.die(c) != topo.die(core))
    return near, far


def _masks(src, cores, topo):
    near, far = _split(src, cores, topo)
    fm, fn, nm, nn = 0, 0, 0, 0
    if far:
        allowed = topo.mask(src, far[0])
        for c in far:
            assert topo.may_write(src, c)
            allowed &= topo.mask(src, c)
        fm, fn = _mask_of(_engines(allowed))
    if near:
        allowed = topo.mask(src, near[0])
        for c in near:
            allowed &= topo.mask(src, c)
        nm, nn = _mask_of(_engines(allowed & ~fm))
    return fm, fn, nm, nn


def rank_program(g, core, T, topo):
    rank = T.rank_of(core)
    if rank is None:
        return
    cores = list(T.cores)
    sem = T.sem
    near, far = _split(core, cores, topo)
    fm, fn, nm, nn = _masks(core, cores, topo)
    lo, hi = PW * rank, PW * rank + PW

    g.sync.dma_start(T.wp[:, lo:hi], T.ws[:]).then_inc(sem.lws, 16)
    g.sync.dma_start(T.wq[:, lo:hi].bitcast(dt.uint8), T.wc[:]).then_inc(sem.lwc, 16)
    g.sync.dma_start(T.xb[:], T.x[:]).then_inc(sem.lx, 16)

    sent = [0]

    def send(view, parts, rsem):
        trs = []
        for dests, m, n in parts:
            ids = []
            for c in dests:
                rid, pid, _se = topo.addr(c)
                ids.append(DstId(rid=rid, pnc=pid))
            trs.append(RemoteDMATransfer(dst_ids=ids, dma_engine_mask=m, remote_sem=rsem,
                                         srcs=[view], dsts=[view for _c in dests]))
            sent[0] += n
        g.remote_dma_fused(trs, local_sem=sem.sent)

    g.wait_ge(sem.lws, 16)
    send(T.wp[:, lo:hi], [(far[:1], fm, fn), (near, nm, nn)], sem["p%d" % rank])
    g.wait_ge(sem.lwc, 16)
    send(T.wq[:, lo:hi].bitcast(dt.uint8), [(far, fm, fn), (near, nm, nn)], sem["a%d" % rank])

    for j, c in enumerate(cores):
        if c == core:
            continue
        _nj, fj = _split(c, cores, topo)
        if fj and fj[0] == core and fj[1:]:
            for d in fj[1:]:
                assert topo.chip(d) == topo.chip(core)
            g.wait_ge(sem["p%d" % j], _masks(c, cores, topo)[1])
            send(T.wp[:, PW * j:PW * j + PW], [(fj[1:], nm, nn)], sem["p%d" % j])

    g.vector.wait_ge(sem.lx, 16)
    g.vector.quantize_mx(T.xq[:], T.xp[:], T.xb[:]).then_inc(sem.q, 1)

    order = [rank] + [T.rank_of(c) for c in near] + [T.rank_of(c) for c in far]

    def landed(j):
        c = cores[j]
        nj, fj = _split(c, cores, topo)
        jfm, jfn, jnm, jnn = _masks(c, cores, topo)
        if core in nj:
            return jnn, jnn
        if core == fj[0]:
            return jfn, jfn
        return jfn, _masks(fj[0], cores, topo)[3]

    g.tensor.wait_ge(sem.lws, 16)
    g.tensor.wait_ge(sem.lwc, 16)
    g.tensor.wait_ge(sem.q, 1)
    for j in order:
        if j != rank:
            na, np_ = landed(j)
            g.tensor.wait_ge(sem["p%d" % j], np_)
            g.tensor.wait_ge(sem["a%d" % j], na)
        for i in range(WT):
            b = WT * j + i
            g.tensor.matmul_mx(T.ps[:, BANK * b:BANK * b + NC], T.wq[:, NC * b:NC * b + NC], T.wp[:, NC * b:NC * b + NC],
                               T.xq[:], T.xp[:], True, True).then_inc(sem["m%d" % b], 1)

    groups = [[rank]] + [[T.rank_of(c)] for c in near] + [[T.rank_of(c)] for c in far]
    last = groups[-1][-1]

    for j in order:
        for i in range(WT):
            b = WT * j + i
            src, dst = T.ps[:, BANK * b:BANK * b + NC], T.yb[:, NC * b:NC * b + NC]
            if i % 2 == 0:
                g.vector.wait_ge(sem["m%d" % b], 1)
                g.vector.tensor_copy(dst, src).then_inc(sem["cp%d" % j], 1)
            else:
                g.scalar.wait_ge(sem["m%d" % b], 1)
                g.scalar.activation(dst, src, ActivationFunctionType.Copy).then_inc(sem["cp%d" % j], 1)

    n_sync = 0
    for grp in groups:
        a, z = PW * min(grp), PW * max(grp) + PW
        if last in grp:
            for j in grp:
                g.scalar.wait_ge(sem["cp%d" % j], WT)
            g.scalar.dma_start(T.y[:, a:z], T.yb[:, a:z]).then_inc(sem.stc, 16)
        else:
            for j in grp:
                g.sync.wait_ge(sem["cp%d" % j], WT)
            g.sync.dma_start(T.y[:, a:z], T.yb[:, a:z]).then_inc(sem.sts, 16)
            n_sync += 1
    if n_sync:
        g.sync.wait_ge(sem.sts, 16 * n_sync)
    g.scalar.wait_ge(sem.stc, 16)

    g.wait_ge(sem.sent, sent[0])
